import numpy as np
import ml_dtypes


def mxq(x, axis, fmt="e4m3"):
    dtype, down = {"e4m3": (ml_dtypes.float8_e4m3fn, 7), "e5m2": (ml_dtypes.float8_e5m2, 14)}[fmt]
    v = np.moveaxis(np.asarray(x, np.float32).astype(ml_dtypes.bfloat16).astype(np.float64), axis, -1)
    blocks = v.reshape(v.shape[:-1] + (-1, 32))
    amax = np.abs(blocks).max(-1, keepdims=True)
    byte = np.maximum(np.where(amax > 0, np.frexp(amax)[1] - 1 + 127, 0) - down, 1)
    scale = np.exp2(byte - 127.0)
    codes = (blocks / scale).astype(np.float32).astype(dtype).astype(np.float64)
    return np.moveaxis((codes * scale).reshape(v.shape), -1, axis)


WIDE = False


def mx_kscale(k):
    if not WIDE:
        return np.ones(k)
    levels = np.array([10, -10, 5, -5, 0])
    if k % 512:
        return np.exp2(np.random.permutation(np.resize(levels, k // 32))).repeat(32)
    a = np.empty((k // 512, 16))
    for p in range(k // 512):
        a[p, :8] = np.random.permutation(np.resize(levels, 8))
        for g in range(8):
            far = levels[np.abs(levels - a[p, g]) >= 10]
            a[p, g + 8] = far[np.random.randint(len(far))]
    return np.exp2(a.ravel()).repeat(32)


def f64(x):
    return np.asarray(x).astype(np.float64)


def striped(idx):
    return np.tile(idx.reshape(-1, 16).T, (8, 1)).astype(np.uint16)


def unstriped(offs):
    return offs[:16].T.reshape(-1).astype(np.int64)


def striped8(idx):
    return np.concatenate([x.reshape(-1, 16).T for x in idx]).astype(np.uint16)


def runs(offs, k):
    lists = np.stack([offs[16 * r : 16 * r + 16].T.reshape(-1) for r in range(8)]).astype(np.int64)
    return lists[np.arange(k) % 512 // 64]


def pack_weight(w):
    k, n = w.shape
    w = f64(np.asarray(w, np.float32).astype(ml_dtypes.bfloat16)).reshape(k // 32, 32, n)
    amax = np.abs(w).max(1)
    byte = np.clip(np.where(amax > 0, np.frexp(amax)[1] - 1 + 127 - 7, 1), 1, 254)
    scaled = (w * np.exp2(127.0 - byte)[:, None, :]).reshape(k, n).astype(np.float32)
    words = np.ascontiguousarray(scaled.reshape(k // 512, 128, 4, n).transpose(0, 1, 3, 2)).astype(ml_dtypes.float8_e4m3fn).view(np.uint8)
    return words, np.ascontiguousarray(byte.astype(np.uint8).reshape(k // 512, 16, n))


def unpack_weight(words, scales):
    g, p, n, _ = words.shape
    vals = np.ascontiguousarray(words).view(ml_dtypes.float8_e4m3fn).astype(np.float64) * np.repeat(np.exp2(scales.astype(np.float64) - 127.0), 8, axis=1)[..., None]
    return vals.transpose(0, 1, 3, 2).reshape(g * 512, n)


def sigmoid(v):
    return 1.0 / (1.0 + np.exp(-np.maximum(v, -700.0)))


K, T, S, N, H = 512, 2048, 512, 512, 512


def setup_inputs():
    n = np.random.standard_normal
    s = mx_kscale(K)[:, None]
    u = mx_kscale(H)
    packed_xT = pack_weight(n((K, T)) * s)
    return {
        "x_words": packed_xT[0],
        "x_scales": packed_xT[1],
        "w1": (n((K, H)) / np.sqrt(K) / s).astype(np.float32),
        "w2": (n((K, H)) / np.sqrt(K) / s).astype(np.float32),
        "gn": (np.random.uniform(0.5, 1.5, (H, 1)) * u[:, None]).astype(np.float32),
        "gm": (np.random.uniform(0.5, 1.5, (H, 1)) * u[:, None]).astype(np.float32),
        "w3": (n((H, N)) / np.sqrt(2 * H) / u[:, None]).astype(np.float32),
        "w4": (n((H, N)) / np.sqrt(2 * H) / u[:, None]).astype(np.float32),
        "offs": striped(np.random.permutation(T)[:S]),
        "hz": striped8(np.random.randint(0, T, (8, S))),
        "n1": striped8(np.stack([np.random.permutation(S) for _ in range(8)])),
        "n2": striped8(np.stack([np.random.permutation(S) for _ in range(8)])),
        "n3": striped8(np.stack([np.random.permutation(S) for _ in range(8)])),
        "n4": striped8(np.stack([np.random.permutation(S) for _ in range(8)])),
        "n5": striped8(np.stack([np.random.permutation(S) for _ in range(8)])),
        "n6": striped8(np.stack([np.random.permutation(S) for _ in range(8)])),
        "n7": striped8(np.stack([np.random.permutation(S) for _ in range(8)])),
        "n8": striped8(np.stack([np.random.permutation(S) for _ in range(8)])),
    }


def reference(x_words, x_scales, w1, w2, gn, gm, w3, w4, offs, hz, n1, n2, n3, n4, n5, n6, n7, n8):
    xq = unpack_weight(x_words, x_scales)[:, unstriped(offs)]
    y = mxq(f64(w1), 0, "e4m3").T @ xq
    b1 = y[np.arange(H)[:, None], runs(n1, H)]
    b2 = y[np.arange(H)[:, None], runs(n2, H)]
    b3 = y[np.arange(H)[:, None], runs(n3, H)]
    z = f64(gn) * (np.maximum(np.maximum(b1, b2), b3) - (0.5 * (np.maximum(np.minimum(b1, b2), np.minimum(np.maximum(b1, b2), b3)))))
    x_hz = unpack_weight(x_words, x_scales)[np.arange(K)[:, None], runs(hz, K)]
    d = mxq(f64(w2), 0, "e4m3").T @ x_hz
    z2 = f64(gm) * ((d * (d[np.arange(H)[:, None], runs(n4, H)])) * (np.tanh(d[np.arange(H)[:, None], runs(n5, H)])))
    h = mxq(f64(w3), 0, "e4m3").T @ mxq(z, 0, "e4m3") + mxq(f64(w4), 0, "e4m3").T @ mxq(z2, 0, "e4m3")
    return (h[np.arange(N)[:, None], runs(n6, N)]) * sigmoid(h) + (h[np.arange(N)[:, None], runs(n7, N)]) * (sigmoid(h[np.arange(N)[:, None], runs(n8, N)]))

@@ -1,0 +1,229 @@
+from contextlib import ExitStack
+
+import concourse.mybir as mybir
+
+F32 = mybir.dt.float32
+BF16 = mybir.dt.bfloat16
+I32 = mybir.dt.int32
+U32 = mybir.dt.uint32
+U16 = mybir.dt.uint16
+U8 = mybir.dt.uint8
+FP8X4 = mybir.dt.float8_e4m3fn_x4
+ALU = mybir.AluOpType
+ACT = mybir.ActivationFunctionType
+
+P = 128
+PACK = 4
+T = 2048
+S = 512
+W = 512
+HALF = S // 2
+FLOPS = 4 * 2 * 512 * 512 * 512
+
+
+def tile_picked_hjointop2cubewsum_none_p_kernel(tc, x_words, x_scales, w1, w2, gn, gm, w3, w4, offs, hz, n1, n2, n3, n4, n5, n6, n7, n8, out):
+    nc = tc.nc
+    with ExitStack() as ctx:
+        keep = ctx.enter_context(tc.tile_pool(name="keep", bufs=1))
+        ring = ctx.enter_context(tc.tile_pool(name="ring", bufs=4))
+        psum = ctx.enter_context(tc.psum_pool(name="psum", bufs=1))
+
+        def load_list(src, name):
+            lst = keep.tile([P, S // 16], U16, name=name)
+            nc.sync.dma_start(lst[:], src)
+            return lst
+
+        def load_weight(w, name, parts):
+            width = W // parts
+            rows = w.rearrange("(p j) c -> p j c", j=PACK)
+            raws = []
+            for a in range(parts):
+                raw = keep.tile([P, PACK, width], F32, name=f"{name}_raw{a}", align_bytes=64)
+                nc.sync.dma_start(raw[:], rows[:, :, a * width : (a + 1) * width])
+                raws.append(raw)
+            return raws
+
+        def cast_weight(raws, name, engines):
+            wb = keep.tile([P, PACK * W], BF16, name=f"{name}_bf", align_bytes=64)
+            dealt = wb[:].rearrange("p (t m j) -> p m j t", t=PACK, j=PACK)
+            step = P // len(raws)
+            for a, (raw, eng) in enumerate(zip(raws, engines)):
+                src = raw[:].rearrange("p j (m t) -> p m j t", t=PACK)
+                dst = dealt[:, a * step : (a + 1) * step]
+                if eng == "scalar":
+                    nc.scalar.copy(dst, src)
+                else:
+                    nc.vector.tensor_copy(dst, src)
+            return wb
+
+        def quantise(src, name, parts=1):
+            codes = keep.tile([P, W], U32, name=f"{name}_codes", align_bytes=64)
+            scales = keep.tile([P, W], U8, name=f"{name}_scales", align_bytes=64)
+            width = W // parts
+            for a in range(parts):
+                cols = slice(a * width, (a + 1) * width)
+                nc.vector.quantize_mx(codes[:, cols].bitcast(FP8X4), scales[:, cols], src[:, PACK * a * width : PACK * (a + 1) * width])
+            return codes, scales
+
+        def product(bank, wq, t, xq, cols, start, stop):
+            rows = slice(t * P, (t + 1) * P)
+            nc.tensor.matmul_mx(bank[:, cols], lhsT=wq[0][:, rows].bitcast(FP8X4), lhsT_scale=wq[1][:, rows],
+                                rhs=xq[0][:, cols].bitcast(FP8X4), rhs_scale=xq[1][:, cols], start=start, stop=stop)
+
+        def halves(lst):
+            return [(slice(h * HALF, (h + 1) * HALF), lst[:, h * HALF // 16 : (h + 1) * HALF // 16]) for h in range(2)]
+
+        def fetch_scalar(dst, window, lst, func=ACT.Copy):
+            for cols, o in halves(lst):
+                nc.scalar.activation(dst[:, cols], window[:].indirect(o), func)
+
+        def fetch_vector(dst, window, lst):
+            for cols, o in halves(lst):
+                nc.vector.tensor_copy(dst[:, cols], window[:].indirect(o))
+
+        def fetch_times(dst, window, lst, other):
+            for cols, o in halves(lst):
+                nc.vector.tensor_tensor(dst[:, cols], window[:].indirect(o), other[:, cols], ALU.mult)
+
+        xs = keep.tile([P, T], U8, name="xs", align_bytes=64)
+        scale_rows = x_scales[0].bitcast(I32)
+        for q in range(4):
+            nc.sync.dma_start(xs[:].bitcast(I32)[32 * q : 32 * q + 32, :],
+                              scale_rows[4 * q : 4 * q + 4, :].unsqueeze(0).broadcast_to([8, 4, T // 4]))
+        hz_t = load_list(hz, "hz_t")
+        offs_t = load_list(offs, "offs_t")
+        xw = keep.tile([P, T], U32, name="xw", align_bytes=64)
+        nc.sync.dma_start(xw[:].bitcast(I32), x_words[0].rearrange("p n t -> p (n t)").bitcast(I32))
+        w1_raw = load_weight(w1, "w1", 2)
+        l1, l2, l3 = load_list(n1, "l1"), load_list(n2, "l2"), load_list(n3, "l3")
+        w2_raw = load_weight(w2, "w2", 1)
+        l4, l5 = load_list(n4, "l4"), load_list(n5, "l5")
+        w3_raw = load_weight(w3, "w3", 1)
+        w4_raw = load_weight(w4, "w4", 1)
+        l6, l7, l8 = load_list(n6, "l6"), load_list(n7, "l7"), load_list(n8, "l8")
+        gn_t = keep.tile([P, PACK], F32, name="gn_t")
+        gm_t = keep.tile([P, PACK], F32, name="gm_t")
+        nc.gpsimd.dma_start(gn_t[:], gn.rearrange("(p t) o -> p (t o)", t=PACK))
+        nc.gpsimd.dma_start(gm_t[:], gm.rearrange("(p t) o -> p (t o)", t=PACK))
+
+        hz_bytes = keep.tile([P, S], U8, name="hz_bytes", align_bytes=64)
+        nc.vector.tensor_copy(hz_bytes[:], xs[:].indirect(hz_t[:]))
+        hz_scales = keep.tile([P, S], U8, name="hz_scales", align_bytes=64)
+        nc.vector.tensor_copy(hz_scales[:].bitcast(I32), hz_bytes[:].bitcast(I32))
+        for r in (2, 3):
+            nc.gpsimd.dma_start(hz_scales[:].bitcast(I32)[r:P:32, :], hz_bytes[:].bitcast(I32)[16 + r : P : 32, :])
+        tok_scales = keep.tile([P, S], U8, name="tok_scales", align_bytes=64)
+        nc.vector.tensor_copy(tok_scales[:], xs[:].indirect(offs_t[:]))
+        tok_words = keep.tile([P, S], U32, name="tok_words", align_bytes=64)
+        nc.vector.tensor_copy(tok_words[:], xw[:].indirect(offs_t[:]))
+
+        everything = slice(0, S)
+        w1_q = quantise(cast_weight(w1_raw, "w1", ("scalar", "vector")), "w1", 2)
+        hz_words = keep.tile([P, S], U32, name="hz_words", tag="w1_raw1", align_bytes=64)
+        nc.vector.tensor_copy(hz_words[:], xw[:].indirect(hz_t[:]))
+        y_banks = [psum.tile([P, S], F32, name=f"y_bank{t}", tag=f"first{t}") for t in range(PACK)]
+        for t in range(PACK):
+            product(y_banks[t], w1_q, t, (tok_words, tok_scales), everything, True, True)
+
+        r4 = keep.tile([P, PACK, S], F32, name="r4")
+
+        def z_fetch(t):
+            y = ring.tile([P, S], F32, name="y")
+            nc.scalar.copy(y[:], y_banks[t][:])
+            b1 = ring.tile([P, S], F32, name="b1")
+            b2 = ring.tile([P, S], F32, name="b2")
+            b3 = ring.tile([P, S], F32, name="b3")
+            fetch_scalar(b1, y, l1)
+            if t == 0:
+                fetch_vector(b2, y, l2)
+            else:
+                fetch_scalar(b2, y, l2)
+            fetch_scalar(b3, y, l3)
+            return b1, b2, b3
+
+        def z_sort(t, b1, b2, b3):
+            hi = ring.tile([P, S], F32, name="hi", bufs=2)
+            lo = ring.tile([P, S], F32, name="lo", bufs=2)
+            nc.vector.tensor_tensor(hi[:], b1[:], b2[:], ALU.max)
+            nc.vector.tensor_tensor(lo[:], b1[:], b2[:], ALU.min)
+            mid = ring.tile([P, S], F32, name="mid", bufs=2)
+            top = ring.tile([P, S], F32, name="top", bufs=2)
+            nc.vector.tensor_tensor(mid[:], hi[:], b3[:], ALU.min)
+            nc.vector.tensor_tensor(top[:], hi[:], b3[:], ALU.max)
+            med = ring.tile([P, S], F32, name="med", bufs=2)
+            nc.vector.tensor_tensor(med[:], lo[:], mid[:], ALU.max)
+            nc.vector.scalar_tensor_tensor(r4[:, t, :], med[:], -0.5, top[:], ALU.mult, ALU.add)
+
+        fetched = z_fetch(0)
+        w2_q = quantise(cast_weight(w2_raw, "w2", ("vector",)), "w2")
+        d_banks = [psum.tile([P, S], F32, name=f"d_bank{t}", tag=f"second{t}") for t in range(PACK)]
+        for t in range(PACK):
+            product(d_banks[t], w2_q, t, (hz_words, hz_scales), everything, True, True)
+        for t in range(PACK):
+            ahead = z_fetch(t + 1) if t + 1 < PACK else None
+            z_sort(t, *fetched)
+            fetched = ahead
+        zb = keep.tile([P, PACK * S], BF16, name="zb", align_bytes=64)
+        nc.vector.tensor_tensor(
+            zb[:].rearrange("p (c i t) -> p c t i", t=PACK, i=4),
+            r4[:].rearrange("p t (c i) -> p c t i", i=4),
+            gn_t[:].unsqueeze(1).unsqueeze(3).broadcast_to([P, S // 4, PACK, 4]), ALU.mult)
+        z_q = quantise(zb, "z")
+
+        q4 = keep.tile([P, PACK, S], F32, name="q4")
+        for t in range(PACK):
+            th = ring.tile([P, S], F32, name="th")
+            nc.scalar.activation(th[:], d_banks[t][:], ACT.Tanh)
+            d = ring.tile([P, S], F32, name="d")
+            nc.scalar.copy(d[:], d_banks[t][:])
+            t5 = ring.tile([P, S], F32, name="t5")
+            fetch_scalar(t5, th, l5)
+            pair = ring.tile([P, S], F32, name="pair", bufs=2)
+            fetch_times(pair, d, l4, t5)
+            nc.vector.scalar_tensor_tensor(q4[:, t, :], d_banks[t][:], gm_t[:, t : t + 1], pair[:], ALU.mult, ALU.mult)
+        w3_q = quantise(cast_weight(w3_raw, "w3", ("scalar",)), "w3")
+        h_banks = [psum.tile([P, S], F32, name=f"h_bank{u}", tag=f"first{u}") for u in range(PACK)]
+        for u in range(PACK):
+            product(h_banks[u], w3_q, u, z_q, everything, True, False)
+        w4_q = quantise(cast_weight(w4_raw, "w4", ("scalar",)), "w4")
+        z2b = keep.tile([P, PACK * S], BF16, name="z2b", align_bytes=64)
+        z2_codes = keep.tile([P, S], U32, name="z2_codes", align_bytes=64)
+        z2_scales = keep.tile([P, S], U8, name="z2_scales", align_bytes=64)
+        for a in range(2):
+            cols = slice(a * HALF, (a + 1) * HALF)
+            nc.vector.tensor_copy(
+                z2b[:, PACK * a * HALF : PACK * (a + 1) * HALF].rearrange("p (c i t) -> p c t i", t=PACK, i=4),
+                q4[:, :, cols].rearrange("p t (c i) -> p c t i", i=4))
+        for a in range(2):
+            cols = slice(a * HALF, (a + 1) * HALF)
+            nc.vector.quantize_mx(z2_codes[:, cols].bitcast(FP8X4), z2_scales[:, cols], z2b[:, PACK * a * HALF : PACK * (a + 1) * HALF])
+        for a in range(2):
+            for t in range(PACK):
+                product(h_banks[t], w4_q, t, (z2_codes, z2_scales), slice(a * HALF, (a + 1) * HALF), False, a == 1)
+
+        out_rows = out.rearrange("(p t) c -> p t c", t=PACK)
+        hs = [ring.tile([P, S], F32, name="h") for t in range(PACK)]
+        sgs = [ring.tile([P, S], F32, name="sg") for t in range(PACK)]
+        nc.scalar.activation(sgs[1][:], h_banks[1][:], ACT.Sigmoid)
+        nc.vector.tensor_copy(hs[0][:], h_banks[0][:])
+        nc.scalar.activation(sgs[0][:], h_banks[0][:], ACT.Sigmoid)
+        nc.vector.tensor_copy(hs[1][:], h_banks[1][:])
+        for t in range(PACK):
+            h, sg = hs[t], sgs[t]
+            if t >= 2:
+                nc.scalar.copy(h[:], h_banks[t][:])
+                nc.scalar.activation(sg[:], h_banks[t][:], ACT.Sigmoid)
+            h7 = ring.tile([P, S], F32, name="h7")
+            fetch_scalar(h7, h, l7)
+            first = ring.tile([P, S], F32, name="first", bufs=2)
+            fetch_times(first, h, l6, sg)
+            second = ring.tile([P, S], F32, name="second", bufs=2)
+            if t % 2 == 1:
+                s8 = ring.tile([P, S], F32, name="s8", bufs=2)
+                fetch_scalar(s8, h, l8, ACT.Sigmoid)
+                nc.vector.tensor_tensor(second[:], s8[:], h7[:], ALU.mult)
+            else:
+                fetch_times(second, sg, l8, h7)
+            res = ring.tile([P, S], F32, name="res", bufs=2)
+            nc.vector.tensor_tensor(res[:], first[:], second[:], ALU.add)
+            nc.sync.dma_start(out_rows[:, t, :], res[:])

@@ -33,27 +33,18 @@ def tile_picked_hjointop2cubewsum_none_p_kernel(tc, x_words, x_scales, w1, w2, g
             nc.sync.dma_start(lst[:], src)
             return lst
 
-        def load_weight(w, name, parts):
-            width = W // parts
-            rows = w.rearrange("(p j) c -> p j c", j=PACK)
-            raws = []
-            for a in range(parts):
-                raw = keep.tile([P, PACK, width], F32, name=f"{name}_raw{a}", align_bytes=64)
-                nc.sync.dma_start(raw[:], rows[:, :, a * width : (a + 1) * width])
-                raws.append(raw)
-            return raws
+        def load_weight(w, name):
+            raw = keep.tile([P, PACK, W], F32, name=f"{name}_raw")
+            nc.sync.dma_start(raw[:], w.rearrange("(p j) c -> p j c", j=PACK))
+            return raw
 
-        def cast_weight(raws, name, engines):
-            wb = keep.tile([P, PACK * W], BF16, name=f"{name}_bf", align_bytes=64)
-            dealt = wb[:].rearrange("p (t m j) -> p m j t", t=PACK, j=PACK)
-            step = P // len(raws)
-            for a, (raw, eng) in enumerate(zip(raws, engines)):
-                src = raw[:].rearrange("p j (m t) -> p m j t", t=PACK)
-                dst = dealt[:, a * step : (a + 1) * step]
-                if eng == "scalar":
-                    nc.scalar.copy(dst, src)
-                else:
-                    nc.vector.tensor_copy(dst, src)
+        def cast_weight(raw, name, copies, tag):
+            wb = keep.tile([P, PACK * W], BF16, name=f"{name}_bf", tag=tag, align_bytes=64)
+            dst = wb[:].rearrange("p (t m j) -> p m j t", t=PACK, j=PACK)
+            src = raw[:].rearrange("p j (m t) -> p m j t", t=PACK)
+            step = P // len(copies)
+            for a, copy in enumerate(copies):
+                copy(dst[:, a * step : (a + 1) * step], src[:, a * step : (a + 1) * step])
             return wb
 
         def quantise(src, name, parts=1):
@@ -70,21 +61,26 @@ def tile_picked_hjointop2cubewsum_none_p_kernel(tc, x_words, x_scales, w1, w2, g
             nc.tensor.matmul_mx(bank[:, cols], lhsT=wq[0][:, rows].bitcast(FP8X4), lhsT_scale=wq[1][:, rows],
                                 rhs=xq[0][:, cols].bitcast(FP8X4), rhs_scale=xq[1][:, cols], start=start, stop=stop)
 
-        def halves(lst):
-            return [(slice(h * HALF, (h + 1) * HALF), lst[:, h * HALF // 16 : (h + 1) * HALF // 16]) for h in range(2)]
-
         def fetch_scalar(dst, window, lst, func=ACT.Copy):
-            for cols, o in halves(lst):
-                nc.scalar.activation(dst[:, cols], window[:].indirect(o), func)
-
-        def fetch_vector(dst, window, lst):
-            for cols, o in halves(lst):
-                nc.vector.tensor_copy(dst[:, cols], window[:].indirect(o))
+            nc.scalar.activation(dst, window[:].indirect(lst[:]), func)
 
         def fetch_times(dst, window, lst, other):
-            for cols, o in halves(lst):
-                nc.vector.tensor_tensor(dst[:, cols], window[:].indirect(o), other[:, cols], ALU.mult)
+            nc.vector.tensor_tensor(dst, window[:].indirect(lst[:]), other, ALU.mult)
 
+        def woven(ap4):
+            return ap4.rearrange("p t (c i) -> p c t i", i=4)
+
+        def weave_target(tile, cols):
+            return tile[:, PACK * cols.start : PACK * cols.stop].rearrange("p (c i t) -> p c t i", t=PACK, i=4)
+
+        first_windows = [keep.tile([P, 2 * S], F32, name=f"first_window{t}") for t in range(PACK)]
+        second_windows = [keep.tile([P, 2 * S], F32, name=f"second_window{t}") for t in range(PACK)]
+        for window in first_windows + second_windows:
+            nc.gpsimd.memset(window[:, S:], 0.0)
+
+        gn_t = keep.tile([P, PACK], F32, name="gn_t")
+        gm_t = keep.tile([P, PACK], F32, name="gm_t")
+        nc.sync.dma_start(gn_t[:], gn.rearrange("(p t) o -> p (t o)", t=PACK))
         xs = keep.tile([P, T], U8, name="xs", align_bytes=64)
         scale_rows = x_scales[0].bitcast(I32)
         for q in range(4):
@@ -92,19 +88,16 @@ def tile_picked_hjointop2cubewsum_none_p_kernel(tc, x_words, x_scales, w1, w2, g
                               scale_rows[4 * q : 4 * q + 4, :].unsqueeze(0).broadcast_to([8, 4, T // 4]))
         hz_t = load_list(hz, "hz_t")
         offs_t = load_list(offs, "offs_t")
+        w1_raw = load_weight(w1, "w1")
         xw = keep.tile([P, T], U32, name="xw", align_bytes=64)
         nc.sync.dma_start(xw[:].bitcast(I32), x_words[0].rearrange("p n t -> p (n t)").bitcast(I32))
-        w1_raw = load_weight(w1, "w1", 2)
         l1, l2, l3 = load_list(n1, "l1"), load_list(n2, "l2"), load_list(n3, "l3")
-        w2_raw = load_weight(w2, "w2", 1)
+        w2_raw = load_weight(w2, "w2")
+        nc.sync.dma_start(gm_t[:], gm.rearrange("(p t) o -> p (t o)", t=PACK))
         l4, l5 = load_list(n4, "l4"), load_list(n5, "l5")
-        w3_raw = load_weight(w3, "w3", 1)
-        w4_raw = load_weight(w4, "w4", 1)
+        w3_raw = load_weight(w3, "w3")
+        w4_raw = load_weight(w4, "w4")
         l6, l7, l8 = load_list(n6, "l6"), load_list(n7, "l7"), load_list(n8, "l8")
-        gn_t = keep.tile([P, PACK], F32, name="gn_t")
-        gm_t = keep.tile([P, PACK], F32, name="gm_t")
-        nc.gpsimd.dma_start(gn_t[:], gn.rearrange("(p t) o -> p (t o)", t=PACK))
-        nc.gpsimd.dma_start(gm_t[:], gm.rearrange("(p t) o -> p (t o)", t=PACK))
 
         hz_bytes = keep.tile([P, S], U8, name="hz_bytes", align_bytes=64)
         nc.vector.tensor_copy(hz_bytes[:], xs[:].indirect(hz_t[:]))
@@ -118,112 +111,129 @@ def tile_picked_hjointop2cubewsum_none_p_kernel(tc, x_words, x_scales, w1, w2, g
         nc.vector.tensor_copy(tok_words[:], xw[:].indirect(offs_t[:]))
 
         everything = slice(0, S)
-        w1_q = quantise(cast_weight(w1_raw, "w1", ("scalar", "vector")), "w1", 2)
-        hz_words = keep.tile([P, S], U32, name="hz_words", tag="w1_raw1", align_bytes=64)
+        w1_q = quantise(cast_weight(w1_raw, "w1", (nc.scalar.copy, nc.vector.tensor_copy), "w1_bf"), "w1", 2)
+        hz_words = keep.tile([P, S], U32, name="hz_words", tag="w1_bf", align_bytes=64)
         nc.vector.tensor_copy(hz_words[:], xw[:].indirect(hz_t[:]))
         y_banks = [psum.tile([P, S], F32, name=f"y_bank{t}", tag=f"first{t}") for t in range(PACK)]
         for t in range(PACK):
             product(y_banks[t], w1_q, t, (tok_words, tok_scales), everything, True, True)
 
-        r4 = keep.tile([P, PACK, S], F32, name="r4")
+        gn_sign = keep.tile([P, PACK], F32, name="gn_sign")
+        gn_step = keep.tile([P, PACK], F32, name="gn_step")
+        gn_size = keep.tile([P, PACK], F32, name="gn_size")
+        nc.vector.tensor_scalar(gn_step[:], gn_t[:], 0.0, 2.0, ALU.is_ge, ALU.mult)
+        nc.vector.tensor_scalar(gn_sign[:], gn_step[:], -1.0, None, ALU.add)
+        nc.vector.tensor_tensor(gn_size[:], gn_t[:], gn_sign[:], ALU.mult)
+
+        a4 = keep.tile([P, PACK, S], F32, name="a4", align_bytes=64)
+        b4 = keep.tile([P, PACK, S], F32, name="b4")
+
+        def y_out(t):
+            nc.scalar.activation(first_windows[t][:, :S], y_banks[t][:], ACT.Copy, scale=gn_size[:, t : t + 1])
 
         def z_fetch(t):
-            y = ring.tile([P, S], F32, name="y")
-            nc.scalar.copy(y[:], y_banks[t][:])
             b1 = ring.tile([P, S], F32, name="b1")
             b2 = ring.tile([P, S], F32, name="b2")
             b3 = ring.tile([P, S], F32, name="b3")
-            fetch_scalar(b1, y, l1)
+            fetch_scalar(b1[:], first_windows[t], l1)
             if t == 0:
-                fetch_vector(b2, y, l2)
+                nc.vector.tensor_copy(b2[:], first_windows[t][:].indirect(l2[:]))
             else:
-                fetch_scalar(b2, y, l2)
-            fetch_scalar(b3, y, l3)
+                fetch_scalar(b2[:], first_windows[t], l2)
+            fetch_scalar(b3[:], first_windows[t], l3)
             return b1, b2, b3
 
         def z_sort(t, b1, b2, b3):
             hi = ring.tile([P, S], F32, name="hi", bufs=2)
             lo = ring.tile([P, S], F32, name="lo", bufs=2)
-            nc.vector.tensor_tensor(hi[:], b1[:], b2[:], ALU.max)
+            rest = ring.tile([P, S], F32, name="rest", bufs=2)
             nc.vector.tensor_tensor(lo[:], b1[:], b2[:], ALU.min)
-            mid = ring.tile([P, S], F32, name="mid", bufs=2)
-            top = ring.tile([P, S], F32, name="top", bufs=2)
-            nc.vector.tensor_tensor(mid[:], hi[:], b3[:], ALU.min)
-            nc.vector.tensor_tensor(top[:], hi[:], b3[:], ALU.max)
-            med = ring.tile([P, S], F32, name="med", bufs=2)
-            nc.vector.tensor_tensor(med[:], lo[:], mid[:], ALU.max)
-            nc.vector.scalar_tensor_tensor(r4[:, t, :], med[:], -0.5, top[:], ALU.mult, ALU.add)
+            nc.vector.tensor_tensor(hi[:], b1[:], b2[:], ALU.max)
+            nc.vector.tensor_tensor(rest[:], lo[:], b3[:], ALU.max)
+            nc.vector.scalar_tensor_tensor(a4[:, t, :], hi[:], -0.5, b3[:], ALU.mult, ALU.add)
+            nc.vector.scalar_tensor_tensor(b4[:, t, :], rest[:], -0.5, hi[:], ALU.mult, ALU.add)
 
-        fetched = z_fetch(0)
-        w2_q = quantise(cast_weight(w2_raw, "w2", ("vector",)), "w2")
-        d_banks = [psum.tile([P, S], F32, name=f"d_bank{t}", tag=f"second{t}") for t in range(PACK)]
+        y_out(0)
+        fetched = []
         for t in range(PACK):
-            product(d_banks[t], w2_q, t, (hz_words, hz_scales), everything, True, True)
-        for t in range(PACK):
-            ahead = z_fetch(t + 1) if t + 1 < PACK else None
-            z_sort(t, *fetched)
-            fetched = ahead
-        zb = keep.tile([P, PACK * S], BF16, name="zb", align_bytes=64)
+            if t + 1 < PACK:
+                y_out(t + 1)
+            fetched.append(z_fetch(t))
+        w2_b = cast_weight(w2_raw, "w2", (nc.vector.tensor_copy,), "w2_bf")
+        w3_b = keep.tile([P, PACK * W], BF16, name="w3_bf", align_bytes=64)
         nc.vector.tensor_tensor(
-            zb[:].rearrange("p (c i t) -> p c t i", t=PACK, i=4),
-            r4[:].rearrange("p t (c i) -> p c t i", i=4),
-            gn_t[:].unsqueeze(1).unsqueeze(3).broadcast_to([P, S // 4, PACK, 4]), ALU.mult)
-        z_q = quantise(zb, "z")
-
-        q4 = keep.tile([P, PACK, S], F32, name="q4")
+            w3_b[:].rearrange("p (t m j) -> p m j t", t=PACK, j=PACK),
+            w3_raw[:].rearrange("p j (m t) -> p m j t", t=PACK),
+            gn_sign[:].unsqueeze(1).unsqueeze(3).broadcast_to([P, P, PACK, PACK]), ALU.mult)
+        w2_q = quantise(w2_b, "w2")
+        QUARTER = S // 4
+        quarters = [slice(b * QUARTER, (b + 1) * QUARTER) for b in range(4)]
+        d_banks = [psum.tile([P, PACK, QUARTER], F32, name=f"d_bank{b}", tag=f"second{b}") for b in range(4)]
         for t in range(PACK):
-            th = ring.tile([P, S], F32, name="th")
-            nc.scalar.activation(th[:], d_banks[t][:], ACT.Tanh)
-            d = ring.tile([P, S], F32, name="d")
-            nc.scalar.copy(d[:], d_banks[t][:])
+            rows = slice(t * P, (t + 1) * P)
+            for b in range(4):
+                nc.tensor.matmul_mx(d_banks[b][:, t, :], lhsT=w2_q[0][:, rows].bitcast(FP8X4), lhsT_scale=w2_q[1][:, rows],
+                                    rhs=hz_words[:, quarters[b]].bitcast(FP8X4), rhs_scale=hz_scales[:, quarters[b]], start=True, stop=True)
+        w3_q = quantise(w3_b, "w3")
+        for t in range(PACK):
+            z_sort(t, *fetched[t])
+        zb = keep.tile([P, PACK * S], BF16, name="zb", align_bytes=64)
+        nc.vector.tensor_tensor(weave_target(zb, everything), woven(a4[:]), woven(b4[:]), ALU.max)
+
+        pair4 = keep.tile([P, PACK, S], F32, name="pair4")
+        for t in range(PACK):
+            for b in range(4):
+                nc.scalar.activation(first_windows[t][:, quarters[b]], d_banks[b][:, t, :], ACT.Tanh)
+            for b in range(4):
+                nc.scalar.activation(second_windows[t][:, quarters[b]], d_banks[b][:, t, :], ACT.Copy, scale=gm_t[:, t : t + 1])
             t5 = ring.tile([P, S], F32, name="t5")
-            fetch_scalar(t5, th, l5)
-            pair = ring.tile([P, S], F32, name="pair", bufs=2)
-            fetch_times(pair, d, l4, t5)
-            nc.vector.scalar_tensor_tensor(q4[:, t, :], d_banks[t][:], gm_t[:, t : t + 1], pair[:], ALU.mult, ALU.mult)
-        w3_q = quantise(cast_weight(w3_raw, "w3", ("scalar",)), "w3")
-        h_banks = [psum.tile([P, S], F32, name=f"h_bank{u}", tag=f"first{u}") for u in range(PACK)]
-        for u in range(PACK):
-            product(h_banks[u], w3_q, u, z_q, everything, True, False)
-        w4_q = quantise(cast_weight(w4_raw, "w4", ("scalar",)), "w4")
+            fetch_scalar(t5[:], first_windows[t], l5)
+            fetch_times(pair4[:, t, :], second_windows[t], l4, t5[:])
+            if t == 0:
+                z_q = quantise(zb, "z")
+                h_banks = [psum.tile([P, S], F32, name=f"h_bank{u}", tag=f"first{u}") for u in range(PACK)]
+                for u in range(PACK):
+                    product(h_banks[u], w3_q, u, z_q, everything, True, False)
+        w4_q = quantise(cast_weight(w4_raw, "w4", (nc.scalar.copy,), "a4"), "w4")
         z2b = keep.tile([P, PACK * S], BF16, name="z2b", align_bytes=64)
         z2_codes = keep.tile([P, S], U32, name="z2_codes", align_bytes=64)
         z2_scales = keep.tile([P, S], U8, name="z2_scales", align_bytes=64)
-        for a in range(2):
-            cols = slice(a * HALF, (a + 1) * HALF)
-            nc.vector.tensor_copy(
-                z2b[:, PACK * a * HALF : PACK * (a + 1) * HALF].rearrange("p (c i t) -> p c t i", t=PACK, i=4),
-                q4[:, :, cols].rearrange("p t (c i) -> p c t i", i=4))
-        for a in range(2):
-            cols = slice(a * HALF, (a + 1) * HALF)
-            nc.vector.quantize_mx(z2_codes[:, cols].bitcast(FP8X4), z2_scales[:, cols], z2b[:, PACK * a * HALF : PACK * (a + 1) * HALF])
-        for a in range(2):
+
+        def z2_quarter(b):
+            cols = quarters[b]
+            nc.vector.quantize_mx(z2_codes[:, cols].bitcast(FP8X4), z2_scales[:, cols], z2b[:, PACK * cols.start : PACK * cols.stop])
             for t in range(PACK):
-                product(h_banks[t], w4_q, t, (z2_codes, z2_scales), slice(a * HALF, (a + 1) * HALF), False, a == 1)
+                product(h_banks[t], w4_q, t, (z2_codes, z2_scales), cols, False, b == 3)
+
+        for b in range(4):
+            nc.vector.tensor_tensor(weave_target(z2b, quarters[b]), woven(d_banks[b][:]), woven(pair4[:, :, quarters[b]]), ALU.mult)
+            if b > 0:
+                z2_quarter(b - 1)
+        z2_quarter(3)
 
         out_rows = out.rearrange("(p t) c -> p t c", t=PACK)
-        hs = [ring.tile([P, S], F32, name="h") for t in range(PACK)]
-        sgs = [ring.tile([P, S], F32, name="sg") for t in range(PACK)]
-        nc.scalar.activation(sgs[1][:], h_banks[1][:], ACT.Sigmoid)
-        nc.vector.tensor_copy(hs[0][:], h_banks[0][:])
-        nc.scalar.activation(sgs[0][:], h_banks[0][:], ACT.Sigmoid)
-        nc.vector.tensor_copy(hs[1][:], h_banks[1][:])
+        hs, sgs = first_windows, second_windows
+        nc.scalar.activation(sgs[1][:, :S], h_banks[1][:], ACT.Sigmoid)
+        nc.vector.tensor_copy(hs[0][:, :S], h_banks[0][:])
+        nc.scalar.activation(sgs[0][:, :S], h_banks[0][:], ACT.Sigmoid)
+        nc.vector.tensor_copy(hs[1][:, :S], h_banks[1][:])
         for t in range(PACK):
             h, sg = hs[t], sgs[t]
             if t >= 2:
-                nc.scalar.copy(h[:], h_banks[t][:])
-                nc.scalar.activation(sg[:], h_banks[t][:], ACT.Sigmoid)
+                nc.scalar.copy(h[:, :S], h_banks[t][:])
+                nc.scalar.activation(sg[:, :S], h_banks[t][:], ACT.Sigmoid)
             h7 = ring.tile([P, S], F32, name="h7")
-            fetch_scalar(h7, h, l7)
+            fetch_scalar(h7[:], h, l7)
             first = ring.tile([P, S], F32, name="first", bufs=2)
-            fetch_times(first, h, l6, sg)
+            fetch_times(first[:], h, l6, sg[:, :S])
             second = ring.tile([P, S], F32, name="second", bufs=2)
             if t % 2 == 1:
                 s8 = ring.tile([P, S], F32, name="s8", bufs=2)
-                fetch_scalar(s8, h, l8, ACT.Sigmoid)
+                fetch_scalar(s8[:], h, l8, ACT.Sigmoid)
                 nc.vector.tensor_tensor(second[:], s8[:], h7[:], ALU.mult)
             else:
-                fetch_times(second, sg, l8, h7)
+                fetch_times(second[:], sg, l8, h7[:])
             res = ring.tile([P, S], F32, name="res", bufs=2)
-            nc.vector.tensor_tensor(res[:], first[:], second[:], ALU.add)
-            nc.sync.dma_start(out_rows[:, t, :], res[:])
+            for cols in (slice(0, HALF), slice(HALF, S)) if t == PACK - 1 else (everything,):
+                nc.vector.tensor_tensor(res[:, cols], first[:, cols], second[:, cols], ALU.add)
+                nc.sync.dma_start(out_rows[:, t, cols], res[:, cols])

@@ -56,16 +56,19 @@ def tile_picked_hjointop2cubewsum_none_p_kernel(tc, x_words, x_scales, w1, w2, g
                 nc.vector.quantize_mx(codes[:, cols].bitcast(FP8X4), scales[:, cols], src[:, PACK * a * width : PACK * (a + 1) * width])
             return codes, scales
 
-        def product(bank, wq, t, xq, cols, start, stop):
+        def product(dst, wq, t, xq, cols, start, stop):
             rows = slice(t * P, (t + 1) * P)
-            nc.tensor.matmul_mx(bank[:, cols], lhsT=wq[0][:, rows].bitcast(FP8X4), lhsT_scale=wq[1][:, rows],
+            nc.tensor.matmul_mx(dst, lhsT=wq[0][:, rows].bitcast(FP8X4), lhsT_scale=wq[1][:, rows],
                                 rhs=xq[0][:, cols].bitcast(FP8X4), rhs_scale=xq[1][:, cols], start=start, stop=stop)
 
-        def fetch_scalar(dst, window, lst, func=ACT.Copy):
-            nc.scalar.activation(dst, window[:].indirect(lst[:]), func)
+        def entries(lst, cols):
+            return lst[:, cols.start // 16 : cols.stop // 16]
 
-        def fetch_times(dst, window, lst, other):
-            nc.vector.tensor_tensor(dst, window[:].indirect(lst[:]), other, ALU.mult)
+        def fetch_scalar(dst, window, lst, func=ACT.Copy, cols=slice(0, S)):
+            nc.scalar.activation(dst, window[:].indirect(entries(lst, cols)), func)
+
+        def fetch_times(dst, window, lst, other, cols=slice(0, S)):
+            nc.vector.tensor_tensor(dst, window[:].indirect(entries(lst, cols)), other, ALU.mult)
 
         def woven(ap4):
             return ap4.rearrange("p t (c i) -> p c t i", i=4)
@@ -77,6 +80,10 @@ def tile_picked_hjointop2cubewsum_none_p_kernel(tc, x_words, x_scales, w1, w2, g
         second_windows = [keep.tile([P, 2 * S], F32, name=f"second_window{t}") for t in range(PACK)]
         for window in first_windows + second_windows:
             nc.gpsimd.memset(window[:, S:], 0.0)
+
+        warm = keep.tile([P, 16], F32, name="warm")
+        nc.vector.memset(warm[:, 0:1], 0.0)
+        nc.scalar.activation(warm[:, 8:9], warm[:, 0:1], ACT.Sigmoid)
 
         gn_t = keep.tile([P, PACK], F32, name="gn_t")
         gm_t = keep.tile([P, PACK], F32, name="gm_t")
@@ -116,7 +123,7 @@ def tile_picked_hjointop2cubewsum_none_p_kernel(tc, x_words, x_scales, w1, w2, g
         nc.vector.tensor_copy(hz_words[:], xw[:].indirect(hz_t[:]))
         y_banks = [psum.tile([P, S], F32, name=f"y_bank{t}", tag=f"first{t}") for t in range(PACK)]
         for t in range(PACK):
-            product(y_banks[t], w1_q, t, (tok_words, tok_scales), everything, True, True)
+            product(y_banks[t][:], w1_q, t, (tok_words, tok_scales), everything, True, True)
 
         gn_sign = keep.tile([P, PACK], F32, name="gn_sign")
         gn_step = keep.tile([P, PACK], F32, name="gn_step")
@@ -136,22 +143,19 @@ def tile_picked_hjointop2cubewsum_none_p_kernel(tc, x_words, x_scales, w1, w2, g
             b2 = ring.tile([P, S], F32, name="b2")
             b3 = ring.tile([P, S], F32, name="b3")
             fetch_scalar(b1[:], first_windows[t], l1)
-            if t == 0:
-                nc.vector.tensor_copy(b2[:], first_windows[t][:].indirect(l2[:]))
-            else:
-                fetch_scalar(b2[:], first_windows[t], l2)
+            fetch_scalar(b2[:], first_windows[t], l2)
             fetch_scalar(b3[:], first_windows[t], l3)
             return b1, b2, b3
 
         def z_sort(t, b1, b2, b3):
-            hi = ring.tile([P, S], F32, name="hi", bufs=2)
-            lo = ring.tile([P, S], F32, name="lo", bufs=2)
+            both = keep.tile([P, 2, S], F32, name="both", tag=("w3_raw", "w4_raw")[t % 2])
+            lo, hi = both[:, 0, :], both[:, 1, :]
             rest = ring.tile([P, S], F32, name="rest", bufs=2)
-            nc.vector.tensor_tensor(lo[:], b1[:], b2[:], ALU.min)
-            nc.vector.tensor_tensor(hi[:], b1[:], b2[:], ALU.max)
-            nc.vector.tensor_tensor(rest[:], lo[:], b3[:], ALU.max)
-            nc.vector.scalar_tensor_tensor(a4[:, t, :], hi[:], -0.5, b3[:], ALU.mult, ALU.add)
-            nc.vector.scalar_tensor_tensor(b4[:, t, :], rest[:], -0.5, hi[:], ALU.mult, ALU.add)
+            nc.vector.tensor_tensor(lo, b1[:], b2[:], ALU.min)
+            nc.vector.tensor_tensor(hi, b1[:], b2[:], ALU.max)
+            nc.vector.tensor_tensor(rest[:], lo, b3[:], ALU.max)
+            nc.vector.scalar_tensor_tensor(a4[:, t, :], hi, -0.5, b3[:], ALU.mult, ALU.add)
+            nc.vector.scalar_tensor_tensor(b4[:, t, :], rest[:], -0.5, hi, ALU.mult, ALU.add)
 
         y_out(0)
         fetched = []
@@ -174,66 +178,127 @@ def tile_picked_hjointop2cubewsum_none_p_kernel(tc, x_words, x_scales, w1, w2, g
             for b in range(4):
                 nc.tensor.matmul_mx(d_banks[b][:, t, :], lhsT=w2_q[0][:, rows].bitcast(FP8X4), lhsT_scale=w2_q[1][:, rows],
                                     rhs=hz_words[:, quarters[b]].bitcast(FP8X4), rhs_scale=hz_scales[:, quarters[b]], start=True, stop=True)
+        z_sort(0, *fetched[0])
+        w4_b = cast_weight(w4_raw, "w4", (nc.vector.tensor_copy,), "w4_bf")
+        z_sort(1, *fetched[1])
         w3_q = quantise(w3_b, "w3")
-        for t in range(PACK):
-            z_sort(t, *fetched[t])
+        w4_q = quantise(w4_b, "w4")
+        z_sort(2, *fetched[2])
+        z_sort(3, *fetched[3])
         zb = keep.tile([P, PACK * S], BF16, name="zb", align_bytes=64)
         nc.vector.tensor_tensor(weave_target(zb, everything), woven(a4[:]), woven(b4[:]), ALU.max)
 
-        pair4 = keep.tile([P, PACK, S], F32, name="pair4")
-        for t in range(PACK):
+        pair4 = keep.tile([P, PACK, S], F32, name="pair4", tag="b4")
+        z2b = keep.tile([P, PACK * S], BF16, name="z2b", align_bytes=64)
+        z2_codes = keep.tile([P, S], U32, name="z2_codes", align_bytes=64)
+        z2_scales = keep.tile([P, S], U8, name="z2_scales", align_bytes=64)
+        t5s = [ring.tile([P, S], F32, name="t5") for t in range(PACK)]
+        left, right = slice(0, HALF), slice(HALF, S)
+
+        def d_out(t):
             for b in range(4):
                 nc.scalar.activation(first_windows[t][:, quarters[b]], d_banks[b][:, t, :], ACT.Tanh)
             for b in range(4):
                 nc.scalar.activation(second_windows[t][:, quarters[b]], d_banks[b][:, t, :], ACT.Copy, scale=gm_t[:, t : t + 1])
-            t5 = ring.tile([P, S], F32, name="t5")
-            fetch_scalar(t5[:], first_windows[t], l5)
-            fetch_times(pair4[:, t, :], second_windows[t], l4, t5[:])
-            if t == 0:
-                z_q = quantise(zb, "z")
-                h_banks = [psum.tile([P, S], F32, name=f"h_bank{u}", tag=f"first{u}") for u in range(PACK)]
-                for u in range(PACK):
-                    product(h_banks[u], w3_q, u, z_q, everything, True, False)
-        w4_q = quantise(cast_weight(w4_raw, "w4", (nc.scalar.copy,), "a4"), "w4")
-        z2b = keep.tile([P, PACK * S], BF16, name="z2b", align_bytes=64)
-        z2_codes = keep.tile([P, S], U32, name="z2_codes", align_bytes=64)
-        z2_scales = keep.tile([P, S], U8, name="z2_scales", align_bytes=64)
+
+        def pair_fused(t, cols):
+            fetch_scalar(t5s[t][:, cols], first_windows[t], l5, cols=cols)
+            fetch_times(pair4[:, t, cols], second_windows[t], l4, t5s[t][:, cols], cols=cols)
+
+        def pair_apart(t, cols):
+            d4 = ring.tile([P, HALF], F32, name="d4", bufs=2)
+            fetch_scalar(t5s[t][:, cols], first_windows[t], l5, cols=cols)
+            fetch_scalar(d4[:], second_windows[t], l4, cols=cols)
+            nc.vector.tensor_tensor(pair4[:, t, cols], d4[:], t5s[t][:, cols], ALU.mult)
+
+        def z2_weave(b):
+            nc.vector.tensor_tensor(weave_target(z2b, quarters[b]), woven(d_banks[b][:]), woven(pair4[:, :, quarters[b]]), ALU.mult)
 
         def z2_quarter(b):
             cols = quarters[b]
             nc.vector.quantize_mx(z2_codes[:, cols].bitcast(FP8X4), z2_scales[:, cols], z2b[:, PACK * cols.start : PACK * cols.stop])
             for t in range(PACK):
-                product(h_banks[t], w4_q, t, (z2_codes, z2_scales), cols, False, b == 3)
+                product(h_part(t, cols), w4_q, t, (z2_codes, z2_scales), cols, False, b % 2 == 1 and t >= 2)
 
-        for b in range(4):
-            nc.vector.tensor_tensor(weave_target(z2b, quarters[b]), woven(d_banks[b][:]), woven(pair4[:, :, quarters[b]]), ALU.mult)
-            if b > 0:
-                z2_quarter(b - 1)
+        d_out(0)
+        pair_fused(0, left)
+        z_q = quantise(zb, "z")
+        h_banks = [psum.tile([P, 2, HALF], F32, name=f"h_bank{u}", tag=f"first{u}") for u in range(PACK)]
+
+        def h_part(t, cols):
+            a = cols.start // HALF
+            return h_banks[2 * a + t % 2][:, t // 2, cols.start - a * HALF : cols.stop - a * HALF]
+
+        for cols in (left, right):
+            for t in range(PACK):
+                product(h_part(t, cols), w3_q, t, z_q, cols, t < 2, False)
+        d_out(1)
+        pair_fused(1, left)
+        d_out(2)
+        pair_fused(2, left)
+        d_out(3)
+        pair_fused(3, left)
+        z2_weave(0)
+        z2_weave(1)
+        z2_quarter(0)
+        z2_quarter(1)
+        pair_fused(0, right)
+        pair_fused(1, right)
+        pair_apart(2, right)
+        pair_apart(3, right)
+        z2_weave(2)
+        z2_weave(3)
+        z2_quarter(2)
         z2_quarter(3)
 
         out_rows = out.rearrange("(p t) c -> p t c", t=PACK)
         hs, sgs = first_windows, second_windows
-        nc.scalar.activation(sgs[1][:, :S], h_banks[1][:], ACT.Sigmoid)
-        nc.vector.tensor_copy(hs[0][:, :S], h_banks[0][:])
-        nc.scalar.activation(sgs[0][:, :S], h_banks[0][:], ACT.Sigmoid)
-        nc.vector.tensor_copy(hs[1][:, :S], h_banks[1][:])
+        firsts = [ring.tile([P, S], F32, name="first") for t in range(PACK)]
+        seconds = [ring.tile([P, S], F32, name="second", bufs=2) for t in range(PACK)]
+        h7s = [ring.tile([P, S], F32, name="h7", bufs=2) for t in range(PACK)]
+        results = [ring.tile([P, S], F32, name="res", bufs=2) for t in range(PACK)]
+
+        def sigmoid_out(t, cols):
+            nc.scalar.activation(sgs[t][:, cols], h_part(t, cols), ACT.Sigmoid)
+
+        def h_out(t, cols):
+            nc.scalar.copy(hs[t][:, cols], h_part(t, cols))
+            sigmoid_out(t, cols)
+
+        def first_term(t):
+            fetch_times(firsts[t][:], hs[t], l6, sgs[t][:, :S])
+
+        def second_apart(t, cols):
+            s8 = ring.tile([P, S], F32, name="s8", bufs=2)
+            fetch_scalar(s8[:, cols], hs[t], l8, ACT.Sigmoid, cols=cols)
+            nc.vector.tensor_tensor(seconds[t][:, cols], s8[:, cols], h7s[t][:, cols], ALU.mult)
+
+        def finish(t, cols):
+            nc.vector.tensor_tensor(results[t][:, cols], firsts[t][:, cols], seconds[t][:, cols], ALU.add)
+            nc.sync.dma_start(out_rows[:, t, cols], results[t][:, cols])
+
         for t in range(PACK):
-            h, sg = hs[t], sgs[t]
-            if t >= 2:
-                nc.scalar.copy(h[:, :S], h_banks[t][:])
-                nc.scalar.activation(sg[:, :S], h_banks[t][:], ACT.Sigmoid)
-            h7 = ring.tile([P, S], F32, name="h7")
-            fetch_scalar(h7[:], h, l7)
-            first = ring.tile([P, S], F32, name="first", bufs=2)
-            fetch_times(first[:], h, l6, sg[:, :S])
-            second = ring.tile([P, S], F32, name="second", bufs=2)
-            if t % 2 == 1:
-                s8 = ring.tile([P, S], F32, name="s8", bufs=2)
-                fetch_scalar(s8[:], h, l8, ACT.Sigmoid)
-                nc.vector.tensor_tensor(second[:], s8[:], h7[:], ALU.mult)
-            else:
-                fetch_times(second[:], sg, l8, h7[:])
-            res = ring.tile([P, S], F32, name="res", bufs=2)
-            for cols in (slice(0, HALF), slice(HALF, S)) if t == PACK - 1 else (everything,):
-                nc.vector.tensor_tensor(res[:, cols], first[:, cols], second[:, cols], ALU.add)
-                nc.sync.dma_start(out_rows[:, t, cols], res[:, cols])
+            h_out(t, left)
+        nc.vector.tensor_copy(hs[0][:, right], h_part(0, right))
+        sigmoid_out(1, right)
+        nc.vector.tensor_copy(hs[1][:, right], h_part(1, right))
+        sigmoid_out(0, right)
+        first_term(0)
+        fetch_scalar(h7s[0][:], hs[0], l7)
+        first_term(1)
+        h_out(2, right)
+        fetch_times(seconds[0][:], sgs[0], l8, h7s[0][:])
+        first_term(2)
+        finish(0, everything)
+        fetch_scalar(h7s[1][:], hs[1], l7)
+        second_apart(1, everything)
+        h_out(3, right)
+        first_term(3)
+        finish(1, everything)
+        fetch_scalar(h7s[2][:], hs[2], l7)
+        second_apart(2, everything)
+        finish(2, everything)
+        fetch_scalar(h7s[3][:], hs[3], l7)
+        for cols in (left, right):
+            second_apart(3, cols)
+            finish(3, cols)

from contextlib import ExitStack

import concourse.mybir as mybir

F32 = mybir.dt.float32
BF16 = mybir.dt.bfloat16
I32 = mybir.dt.int32
U32 = mybir.dt.uint32
U16 = mybir.dt.uint16
U8 = mybir.dt.uint8
FP8X4 = mybir.dt.float8_e4m3fn_x4
ALU = mybir.AluOpType
ACT = mybir.ActivationFunctionType

P = 128
PACK = 4
T = 2048
S = 512
W = 512
HALF = S // 2
FLOPS = 4 * 2 * 512 * 512 * 512


def tile_picked_hjointop2cubewsum_none_p_kernel(tc, x_words, x_scales, w1, w2, gn, gm, w3, w4, offs, hz, n1, n2, n3, n4, n5, n6, n7, n8, out):
    nc = tc.nc
    with ExitStack() as ctx:
        keep = ctx.enter_context(tc.tile_pool(name="keep", bufs=1))
        ring = ctx.enter_context(tc.tile_pool(name="ring", bufs=4))
        psum = ctx.enter_context(tc.psum_pool(name="psum", bufs=1))

        def load_list(src, name):
            lst = keep.tile([P, S // 16], U16, name=name)
            nc.sync.dma_start(lst[:], src)
            return lst

        def load_weight(w, name):
            raw = keep.tile([P, PACK, W], F32, name=f"{name}_raw")
            nc.sync.dma_start(raw[:], w.rearrange("(p j) c -> p j c", j=PACK))
            return raw

        def cast_weight(raw, name, copies, tag):
            wb = keep.tile([P, PACK * W], BF16, name=f"{name}_bf", tag=tag, align_bytes=64)
            dst = wb[:].rearrange("p (t m j) -> p m j t", t=PACK, j=PACK)
            src = raw[:].rearrange("p j (m t) -> p m j t", t=PACK)
            step = P // len(copies)
            for a, copy in enumerate(copies):
                copy(dst[:, a * step : (a + 1) * step], src[:, a * step : (a + 1) * step])
            return wb

        def quantise(src, name, parts=1):
            codes = keep.tile([P, W], U32, name=f"{name}_codes", align_bytes=64)
            scales = keep.tile([P, W], U8, name=f"{name}_scales", align_bytes=64)
            width = W // parts
            for a in range(parts):
                cols = slice(a * width, (a + 1) * width)
                nc.vector.quantize_mx(codes[:, cols].bitcast(FP8X4), scales[:, cols], src[:, PACK * a * width : PACK * (a + 1) * width])
            return codes, scales

        def product(dst, wq, t, xq, cols, start, stop):
            rows = slice(t * P, (t + 1) * P)
            nc.tensor.matmul_mx(dst, lhsT=wq[0][:, rows].bitcast(FP8X4), lhsT_scale=wq[1][:, rows],
                                rhs=xq[0][:, cols].bitcast(FP8X4), rhs_scale=xq[1][:, cols], start=start, stop=stop)

        def entries(lst, cols):
            return lst[:, cols.start // 16 : cols.stop // 16]

        def fetch_scalar(dst, window, lst, func=ACT.Copy, cols=slice(0, S)):
            nc.scalar.activation(dst, window[:].indirect(entries(lst, cols)), func)

        def fetch_times(dst, window, lst, other, cols=slice(0, S)):
            nc.vector.tensor_tensor(dst, window[:].indirect(entries(lst, cols)), other, ALU.mult)

        def woven(ap4):
            return ap4.rearrange("p t (c i) -> p c t i", i=4)

        def weave_target(tile, cols):
            return tile[:, PACK * cols.start : PACK * cols.stop].rearrange("p (c i t) -> p c t i", t=PACK, i=4)

        first_windows = [keep.tile([P, 2 * S], F32, name=f"first_window{t}") for t in range(PACK)]
        second_windows = [keep.tile([P, 2 * S], F32, name=f"second_window{t}") for t in range(PACK)]
        for window in first_windows + second_windows:
            nc.gpsimd.memset(window[:, S:], 0.0)

        warm = keep.tile([P, 16], F32, name="warm")
        nc.vector.memset(warm[:, 0:1], 0.0)
        nc.scalar.activation(warm[:, 8:9], warm[:, 0:1], ACT.Sigmoid)

        gn_t = keep.tile([P, PACK], F32, name="gn_t")
        gm_t = keep.tile([P, PACK], F32, name="gm_t")
        nc.sync.dma_start(gn_t[:], gn.rearrange("(p t) o -> p (t o)", t=PACK))
        xs = keep.tile([P, T], U8, name="xs", align_bytes=64)
        scale_rows = x_scales[0].bitcast(I32)
        for q in range(4):
            nc.sync.dma_start(xs[:].bitcast(I32)[32 * q : 32 * q + 32, :],
                              scale_rows[4 * q : 4 * q + 4, :].unsqueeze(0).broadcast_to([8, 4, T // 4]))
        hz_t = load_list(hz, "hz_t")
        offs_t = load_list(offs, "offs_t")
        w1_raw = load_weight(w1, "w1")
        xw = keep.tile([P, T], U32, name="xw", align_bytes=64)
        nc.sync.dma_start(xw[:].bitcast(I32), x_words[0].rearrange("p n t -> p (n t)").bitcast(I32))
        l1, l2, l3 = load_list(n1, "l1"), load_list(n2, "l2"), load_list(n3, "l3")
        w2_raw = load_weight(w2, "w2")
        nc.sync.dma_start(gm_t[:], gm.rearrange("(p t) o -> p (t o)", t=PACK))
        l4, l5 = load_list(n4, "l4"), load_list(n5, "l5")
        w3_raw = load_weight(w3, "w3")
        w4_raw = load_weight(w4, "w4")
        l6, l7, l8 = load_list(n6, "l6"), load_list(n7, "l7"), load_list(n8, "l8")

        hz_bytes = keep.tile([P, S], U8, name="hz_bytes", align_bytes=64)
        nc.vector.tensor_copy(hz_bytes[:], xs[:].indirect(hz_t[:]))
        hz_scales = keep.tile([P, S], U8, name="hz_scales", align_bytes=64)
        nc.vector.tensor_copy(hz_scales[:].bitcast(I32), hz_bytes[:].bitcast(I32))
        for r in (2, 3):
            nc.gpsimd.dma_start(hz_scales[:].bitcast(I32)[r:P:32, :], hz_bytes[:].bitcast(I32)[16 + r : P : 32, :])
        tok_scales = keep.tile([P, S], U8, name="tok_scales", align_bytes=64)
        nc.vector.tensor_copy(tok_scales[:], xs[:].indirect(offs_t[:]))
        tok_words = keep.tile([P, S], U32, name="tok_words", align_bytes=64)
        nc.vector.tensor_copy(tok_words[:], xw[:].indirect(offs_t[:]))

        everything = slice(0, S)
        w1_q = quantise(cast_weight(w1_raw, "w1", (nc.scalar.copy, nc.vector.tensor_copy), "w1_bf"), "w1", 2)
        hz_words = keep.tile([P, S], U32, name="hz_words", tag="w1_bf", align_bytes=64)
        nc.vector.tensor_copy(hz_words[:], xw[:].indirect(hz_t[:]))
        y_banks = [psum.tile([P, S], F32, name=f"y_bank{t}", tag=f"first{t}") for t in range(PACK)]
        for t in range(PACK):
            product(y_banks[t][:], w1_q, t, (tok_words, tok_scales), everything, True, True)

        gn_sign = keep.tile([P, PACK], F32, name="gn_sign")
        gn_step = keep.tile([P, PACK], F32, name="gn_step")
        gn_size = keep.tile([P, PACK], F32, name="gn_size")
        nc.vector.tensor_scalar(gn_step[:], gn_t[:], 0.0, 2.0, ALU.is_ge, ALU.mult)
        nc.vector.tensor_scalar(gn_sign[:], gn_step[:], -1.0, None, ALU.add)
        nc.vector.tensor_tensor(gn_size[:], gn_t[:], gn_sign[:], ALU.mult)

        a4 = keep.tile([P, PACK, S], F32, name="a4", align_bytes=64)
        b4 = keep.tile([P, PACK, S], F32, name="b4")

        def y_out(t):
            nc.scalar.activation(first_windows[t][:, :S], y_banks[t][:], ACT.Copy, scale=gn_size[:, t : t + 1])

        def z_fetch(t):
            b1 = ring.tile([P, S], F32, name="b1")
            b2 = ring.tile([P, S], F32, name="b2")
            b3 = ring.tile([P, S], F32, name="b3")
            fetch_scalar(b1[:], first_windows[t], l1)
            fetch_scalar(b2[:], first_windows[t], l2)
            fetch_scalar(b3[:], first_windows[t], l3)
            return b1, b2, b3

        def z_sort(t, b1, b2, b3):
            both = keep.tile([P, 2, S], F32, name="both", tag=("w3_raw", "w4_raw")[t % 2])
            lo, hi = both[:, 0, :], both[:, 1, :]
            rest = ring.tile([P, S], F32, name="rest", bufs=2)
            nc.vector.tensor_tensor(lo, b1[:], b2[:], ALU.min)
            nc.vector.tensor_tensor(hi, b1[:], b2[:], ALU.max)
            nc.vector.tensor_tensor(rest[:], lo, b3[:], ALU.max)
            nc.vector.scalar_tensor_tensor(a4[:, t, :], hi, -0.5, b3[:], ALU.mult, ALU.add)
            nc.vector.scalar_tensor_tensor(b4[:, t, :], rest[:], -0.5, hi, ALU.mult, ALU.add)

        y_out(0)
        fetched = []
        for t in range(PACK):
            if t + 1 < PACK:
                y_out(t + 1)
            fetched.append(z_fetch(t))
        w2_b = cast_weight(w2_raw, "w2", (nc.vector.tensor_copy,), "w2_bf")
        w3_b = keep.tile([P, PACK * W], BF16, name="w3_bf", align_bytes=64)
        nc.vector.tensor_tensor(
            w3_b[:].rearrange("p (t m j) -> p m j t", t=PACK, j=PACK),
            w3_raw[:].rearrange("p j (m t) -> p m j t", t=PACK),
            gn_sign[:].unsqueeze(1).unsqueeze(3).broadcast_to([P, P, PACK, PACK]), ALU.mult)
        w2_q = quantise(w2_b, "w2")
        QUARTER = S // 4
        quarters = [slice(b * QUARTER, (b + 1) * QUARTER) for b in range(4)]
        d_banks = [psum.tile([P, PACK, QUARTER], F32, name=f"d_bank{b}", tag=f"second{b}") for b in range(4)]
        for t in range(PACK):
            rows = slice(t * P, (t + 1) * P)
            for b in range(4):
                nc.tensor.matmul_mx(d_banks[b][:, t, :], lhsT=w2_q[0][:, rows].bitcast(FP8X4), lhsT_scale=w2_q[1][:, rows],
                                    rhs=hz_words[:, quarters[b]].bitcast(FP8X4), rhs_scale=hz_scales[:, quarters[b]], start=True, stop=True)
        z_sort(0, *fetched[0])
        w4_b = cast_weight(w4_raw, "w4", (nc.vector.tensor_copy,), "w4_bf")
        z_sort(1, *fetched[1])
        w3_q = quantise(w3_b, "w3")
        w4_q = quantise(w4_b, "w4")
        z_sort(2, *fetched[2])
        z_sort(3, *fetched[3])
        zb = keep.tile([P, PACK * S], BF16, name="zb", align_bytes=64)
        nc.vector.tensor_tensor(weave_target(zb, everything), woven(a4[:]), woven(b4[:]), ALU.max)

        pair4 = keep.tile([P, PACK, S], F32, name="pair4", tag="b4")
        z2b = keep.tile([P, PACK * S], BF16, name="z2b", align_bytes=64)
        z2_codes = keep.tile([P, S], U32, name="z2_codes", align_bytes=64)
        z2_scales = keep.tile([P, S], U8, name="z2_scales", align_bytes=64)
        t5s = [ring.tile([P, S], F32, name="t5") for t in range(PACK)]
        left, right = slice(0, HALF), slice(HALF, S)

        def d_out(t):
            for b in range(4):
                nc.scalar.activation(first_windows[t][:, quarters[b]], d_banks[b][:, t, :], ACT.Tanh)
            for b in range(4):
                nc.scalar.activation(second_windows[t][:, quarters[b]], d_banks[b][:, t, :], ACT.Copy, scale=gm_t[:, t : t + 1])

        def pair_fused(t, cols):
            fetch_scalar(t5s[t][:, cols], first_windows[t], l5, cols=cols)
            fetch_times(pair4[:, t, cols], second_windows[t], l4, t5s[t][:, cols], cols=cols)

        def pair_apart(t, cols):
            d4 = ring.tile([P, HALF], F32, name="d4", bufs=2)
            fetch_scalar(t5s[t][:, cols], first_windows[t], l5, cols=cols)
            fetch_scalar(d4[:], second_windows[t], l4, cols=cols)
            nc.vector.tensor_tensor(pair4[:, t, cols], d4[:], t5s[t][:, cols], ALU.mult)

        def z2_weave(b):
            nc.vector.tensor_tensor(weave_target(z2b, quarters[b]), woven(d_banks[b][:]), woven(pair4[:, :, quarters[b]]), ALU.mult)

        def z2_quarter(b):
            cols = quarters[b]
            nc.vector.quantize_mx(z2_codes[:, cols].bitcast(FP8X4), z2_scales[:, cols], z2b[:, PACK * cols.start : PACK * cols.stop])
            for t in range(PACK):
                product(h_part(t, cols), w4_q, t, (z2_codes, z2_scales), cols, False, b % 2 == 1 and t >= 2)

        d_out(0)
        pair_fused(0, left)
        z_q = quantise(zb, "z")
        h_banks = [psum.tile([P, 2, HALF], F32, name=f"h_bank{u}", tag=f"first{u}") for u in range(PACK)]

        def h_part(t, cols):
            a = cols.start // HALF
            return h_banks[2 * a + t % 2][:, t // 2, cols.start - a * HALF : cols.stop - a * HALF]

        for cols in (left, right):
            for t in range(PACK):
                product(h_part(t, cols), w3_q, t, z_q, cols, t < 2, False)
        d_out(1)
        pair_fused(1, left)
        d_out(2)
        pair_fused(2, left)
        d_out(3)
        pair_fused(3, left)
        z2_weave(0)
        z2_weave(1)
        z2_quarter(0)
        z2_quarter(1)
        pair_fused(0, right)
        pair_fused(1, right)
        pair_apart(2, right)
        pair_apart(3, right)
        z2_weave(2)
        z2_weave(3)
        z2_quarter(2)
        z2_quarter(3)

        out_rows = out.rearrange("(p t) c -> p t c", t=PACK)
        hs, sgs = first_windows, second_windows
        firsts = [ring.tile([P, S], F32, name="first") for t in range(PACK)]
        seconds = [ring.tile([P, S], F32, name="second", bufs=2) for t in range(PACK)]
        h7s = [ring.tile([P, S], F32, name="h7", bufs=2) for t in range(PACK)]
        results = [ring.tile([P, S], F32, name="res", bufs=2) for t in range(PACK)]

        def sigmoid_out(t, cols):
            nc.scalar.activation(sgs[t][:, cols], h_part(t, cols), ACT.Sigmoid)

        def h_out(t, cols):
            nc.scalar.copy(hs[t][:, cols], h_part(t, cols))
            sigmoid_out(t, cols)

        def first_term(t):
            fetch_times(firsts[t][:], hs[t], l6, sgs[t][:, :S])

        def second_apart(t, cols):
            s8 = ring.tile([P, S], F32, name="s8", bufs=2)
            fetch_scalar(s8[:, cols], hs[t], l8, ACT.Sigmoid, cols=cols)
            nc.vector.tensor_tensor(seconds[t][:, cols], s8[:, cols], h7s[t][:, cols], ALU.mult)

        def finish(t, cols):
            nc.vector.tensor_tensor(results[t][:, cols], firsts[t][:, cols], seconds[t][:, cols], ALU.add)
            nc.sync.dma_start(out_rows[:, t, cols], results[t][:, cols])

        for t in range(PACK):
            h_out(t, left)
        nc.vector.tensor_copy(hs[0][:, right], h_part(0, right))
        sigmoid_out(1, right)
        nc.vector.tensor_copy(hs[1][:, right], h_part(1, right))
        sigmoid_out(0, right)
        first_term(0)
        fetch_scalar(h7s[0][:], hs[0], l7)
        first_term(1)
        h_out(2, right)
        fetch_times(seconds[0][:], sgs[0], l8, h7s[0][:])
        first_term(2)
        finish(0, everything)
        fetch_scalar(h7s[1][:], hs[1], l7)
        second_apart(1, everything)
        h_out(3, right)
        first_term(3)
        finish(1, everything)
        fetch_scalar(h7s[2][:], hs[2], l7)
        second_apart(2, everything)
        finish(2, everything)
        fetch_scalar(h7s[3][:], hs[3], l7)
        for cols in (left, right):
            second_apart(3, cols)
            finish(3, cols)
